import numpy as np
import ml_dtypes

BF16 = ml_dtypes.bfloat16


def bf(x):
    return np.asarray(x, np.float32).astype(BF16)


def f32(x):
    return np.asarray(x, np.float32)


def f64(x):
    return np.asarray(x).astype(np.float64)


def striped(idx):
    return np.concatenate([l.reshape(-1, 16).T for l in idx])


def rows(idx, k):
    return np.tile(np.repeat(idx, 16, axis=0), (k // (16 * 8), 1))


def look(tab, idx):
    return np.take_along_axis(f64(tab), rows(idx, len(tab)), axis=1)


K, S, D, V, N = 128, 2048, 3, 512, 1536


def setup_inputs():
    return {"tab": f32(np.random.standard_normal((K, S))), "x0": f32(np.random.standard_normal((K, V))), "offs": striped(np.stack([np.random.permutation(S)[:N] for _ in range(8)]))}


def reference(tab, x0, offs):
    idx = np.stack([g.T.reshape(-1) for g in np.split(offs, 8)])
    x = f64(x0)
    for d in range(D):
        x = np.maximum(x, look(tab, idx[:, d * V:(d + 1) * V]))
    return x

import concourse.mybir as mybir

F32 = mybir.dt.float32
U16 = mybir.dt.uint16
MAX = mybir.AluOpType.max

ROWS = 128
COLUMNS = 2048
NEIGHBOURS = 3
POINTS = 512
LIST_COLUMNS = NEIGHBOURS * POINTS // 16
PIECE_COLUMNS = POINTS // 16

FLOPS = NEIGHBOURS * ROWS * POINTS


def tile_lookup_pool_max_out_kernel(tc, tab, x0, offs, out):
    nc = tc.nc
    with tc.tile_pool(name="held", bufs=1) as held:
        offsets = held.tile([ROWS, LIST_COLUMNS], U16, name="offsets")
        table = held.tile([ROWS, COLUMNS], F32, name="table")
        centre = held.tile([ROWS, POINTS], F32, name="centre")

        nc.scalar.dma_start(table[:], tab)
        nc.sync.dma_start(offsets[:], offs)
        nc.sync.dma_start(centre[:], x0)

        largest = centre
        for d in range(NEIGHBOURS):
            pick = offsets[:, d * PIECE_COLUMNS : (d + 1) * PIECE_COLUMNS]
            larger = held.tile([ROWS, POINTS], F32, name=f"largest{d}")
            nc.vector.tensor_tensor(larger[:], table[:].indirect(pick), largest[:], MAX)
            largest = larger

        nc.sync.dma_start(out, largest[:])
